import numpy as np
import ml_dtypes


def mxq(x, axis, fmt="e4m3"):
    dtype, down = {"e4m3": (ml_dtypes.float8_e4m3fn, 7), "e5m2": (ml_dtypes.float8_e5m2, 14)}[fmt]
    v = np.moveaxis(np.asarray(x, np.float32).astype(ml_dtypes.bfloat16).astype(np.float64), axis, -1)
    blocks = v.reshape(v.shape[:-1] + (-1, 32))
    amax = np.abs(blocks).max(-1, keepdims=True)
    byte = np.maximum(np.where(amax > 0, np.frexp(amax)[1] - 1 + 127, 0) - down, 1)
    scale = np.exp2(byte - 127.0)
    codes = (blocks / scale).astype(np.float32).astype(dtype).astype(np.float64)
    return np.moveaxis((codes * scale).reshape(v.shape), -1, axis)


WIDE = False


def mx_kscale(k):
    if not WIDE:
        return np.ones(k)
    levels = np.array([10, -10, 5, -5, 0])
    if k % 512:
        return np.exp2(np.random.permutation(np.resize(levels, k // 32))).repeat(32)
    a = np.empty((k // 512, 16))
    for p in range(k // 512):
        a[p, :8] = np.random.permutation(np.resize(levels, 8))
        for g in range(8):
            far = levels[np.abs(levels - a[p, g]) >= 10]
            a[p, g + 8] = far[np.random.randint(len(far))]
    return np.exp2(a.ravel()).repeat(32)


BF16 = ml_dtypes.bfloat16


def bf(x):
    return np.asarray(x, np.float32).astype(BF16)


def f64(x):
    return np.asarray(x).astype(np.float64)


N1, N2, J1, J2 = 1024, 2048, 1024, 512


def draw0():
    s, t = mx_kscale(J2), mx_kscale(J1)
    k1 = np.random.standard_normal((N1, J1)) / np.sqrt(J1) / t
    dist = np.random.standard_normal((J1, J2)) * s
    k2 = np.random.standard_normal((N2, J2)) / np.sqrt(J2) / s
    pol = np.random.uniform(0.5, 1.0, J1) * t
    data = np.random.standard_normal((N1, N2))
    wt = np.random.uniform(0.5, 1.5, N2)
    return {"k1": bf(k1), "dist": bf(dist), "k2": bf(k2),
            "pol": bf(pol), "data": bf(data), "wt": bf(wt)}


def core(k1, dist, k2, pol, data, wt):
    fq = mxq(f64(dist), 1, "e4m3")
    k2q = mxq(f64(k2), 1, "e4m3")
    g = fq @ k2q.T
    h = g * f64(pol)[:, None]
    k1q = mxq(f64(k1), 1, "e4m3")
    hq = mxq(h, 0, "e4m3")
    signal = k1q @ hq
    return (signal - f64(data)) * f64(wt)[None, :]


def e4m3fn_bytes(y):
    return np.clip(np.asarray(y, np.float64), -448.0, 448.0).astype(np.float32).astype(ml_dtypes.float8_e4m3fn).view(np.uint8)


def e4m3fn_values(b):
    return np.asarray(b, np.uint8).view(ml_dtypes.float8_e4m3fn).astype(np.float64)


def setup_inputs():
    d = draw0()
    x0 = np.asarray(d['k2']).astype(np.float64)
    s = (np.max(np.abs(x0), axis=(0,), keepdims=True) / 448.0).astype(np.float32)
    out = {}
    for k, v in d.items():
        if k == 'k2':
            out['k2_bytes'] = e4m3fn_bytes(x0 / s.astype(np.float64))
            out['k2_scale'] = s
        else:
            out[k] = v
    return out


def reference(k1, dist, k2_bytes, k2_scale, pol, data, wt):
    return core(k1, dist, e4m3fn_values(k2_bytes) * k2_scale.astype(np.float64), pol, data, wt)

from contextlib import ExitStack

import concourse.mybir as mybir
from concourse.masks import make_identity

N1, N2, J1, J2 = 1024, 2048, 1024, 512
FLOPS = 2 * J1 * N2 * J2 + 2 * N1 * N2 * J1

F32 = mybir.dt.float32
BF16 = mybir.dt.bfloat16
U32 = mybir.dt.uint32
U8 = mybir.dt.uint8
FP8 = mybir.dt.float8_e4m3fn
FP8X4 = mybir.dt.float8_e4m3fn_x4
MULT = mybir.AluOpType.mult
SUB = mybir.AluOpType.subtract
COPY = mybir.ActivationFunctionType.Copy

P = 128
NB = 512
BLOCKS = N2 // NB
ITILES = N1 // P
GROUPS = J1 // 512


def tile_nmr_relaxometry_residual_s7_kernel(tc, k1, dist, k2_bytes, k2_scale, pol, data, wt, out):
    nc = tc.nc
    with ExitStack() as ctx:
        keep = ctx.enter_context(tc.tile_pool(name="keep", bufs=1))
        wide = ctx.enter_context(tc.tile_pool(name="wide", bufs=2))
        hpool = ctx.enter_context(tc.tile_pool(name="hpool", bufs=3))
        hcpool = ctx.enter_context(tc.tile_pool(name="hcpool", bufs=4))
        opool = ctx.enter_context(tc.tile_pool(name="opool", bufs=8))
        ps_tr = ctx.enter_context(tc.psum_pool(name="ps_tr", bufs=2))
        ps_g = ctx.enter_context(tc.psum_pool(name="ps_g", bufs=3))
        ps_s = ctx.enter_context(tc.psum_pool(name="ps_s", bufs=3))

        ident = keep.tile([P, P], F32, name="ident")
        make_identity(nc, ident[:])

        ks = keep.tile([P, 4], F32, name="ks")
        nc.sync.dma_start(out=ks[:], in_=k2_scale.rearrange("o (p c) -> p (o c)", c=4))
        kbytes, dsb, k1sb, dat = {}, {}, {}, {}
        wt_bc = keep.tile([P, N2], BF16, name="wt_bc")
        polb = keep.tile([P, 8], BF16, name="polb")
        polf = keep.tile([P, 8], F32, name="polf")

        def load_k2(b):
            kbytes[b] = keep.tile([P, 4, J2], U8, name="kbytes%d" % b)
            nc.sync.dma_start(out=kbytes[b][:], in_=k2_bytes[b * NB : (b + 1) * NB, :].rearrange("(r p) l -> p r l", p=P))

        def load_dist(g):
            dsb[g] = keep.tile([P, 4 * J2], BF16, name="dsb%d" % g)
            nc.sync.dma_start(out=dsb[g][:], in_=dist[g * 512 : (g + 1) * 512, :].rearrange("(p t) l -> p (t l)", t=4))

        def load_k1(i):
            k1sb[i] = keep.tile([P, J1], BF16, name="k1sb%d" % i)
            nc.sync.dma_start(out=k1sb[i][:], in_=k1[i * P : (i + 1) * P, :])

        def load_data(b, h):
            dat[b, h] = keep.tile([P, 4, NB], BF16, name="dat%d_%d" % (b, h))
            nc.sync.dma_start(
                out=dat[b, h][:],
                in_=data[h * 512 : (h + 1) * 512, b * NB : (b + 1) * NB].rearrange("(i p) m -> p i m", p=P),
            )

        def load_wt(b):
            nc.sync.dma_start(out=wt_bc[:, b * NB : (b + 1) * NB], in_=wt[b * NB : (b + 1) * NB].partition_broadcast(P))

        load_k2(0)
        load_dist(0)
        load_dist(1)
        nc.sync.dma_start(out=polb[:].rearrange("p (g t) -> p g t", t=4), in_=pol.rearrange("(g p t) -> p g t", p=P, t=4))
        load_k2(1)
        load_k1(0)
        load_k1(1)
        load_k2(2)
        load_k1(2)
        load_k1(3)
        load_data(0, 0)
        load_wt(0)
        load_k1(4)
        load_k1(5)
        load_data(0, 1)
        load_k1(6)
        load_k1(7)
        load_k2(3)
        for b in range(1, BLOCKS):
            load_wt(b)
            load_data(b, 0)
            load_data(b, 1)

        psum, k2w, kg, kcodes, kscales = {}, {}, {}, {}, {}
        dg, dcodes, dscales, k1g, k1codes, k1scales = {}, {}, {}, {}, {}, {}
        hp, hi, hcodes, hscales, res = {}, {}, {}, {}, {}
        scale_bc = keep.tile([P, J2], F32, name="scale_bc")

        def evict_words(eng, dst, src):
            if eng == "S":
                nc.scalar.copy(out=dst, in_=src)
            else:
                nc.vector.tensor_copy(out=dst, in_=src)

        def scale_bcast():
            ps = ps_tr.tile([P, 4, P], F32, name="tr")
            for c in range(4):
                nc.tensor.transpose(ps[:, c, :], ks[:, c : c + 1].to_broadcast([P, P]), ident[:])
            nc.vector.tensor_copy(out=scale_bc[:].rearrange("p (n c) -> p n c", c=4), in_=ps[:].rearrange("p c n -> p n c"))

        def widen(b, r):
            if r == 0:
                k2w[b] = wide.tile([P, 4, J2], BF16, name="k2w")
            nc.vector.tensor_tensor(out=k2w[b][:, r, :], in0=kbytes[b][:, r, :].bitcast(FP8), in1=scale_bc[:], op=MULT)

        def widen_sg(b):
            raw = wide.tile([P, 4, J2], BF16, name="k2raw")
            nc.scalar.copy(out=raw[:].rearrange("p r l -> p (r l)"), in_=kbytes[b][:].rearrange("p r l -> p (r l)").bitcast(FP8))
            k2w[b] = wide.tile([P, 4, J2], BF16, name="k2w")
            for r in range(4):
                nc.gpsimd.tensor_tensor(out=k2w[b][:, r, :], in0=raw[:, r, :], in1=scale_bc[:], op=MULT)

        def pair_transposes(key, words, offs):
            ps = ps_tr.tile([P, 2, 2, P], F32, name="tr")
            psum[key] = ps
            for a, off in enumerate(offs):
                for u in (0, 1):
                    nc.tensor.transpose(ps[:, a, u, :], words[:, off + u : off + 256 : 2], ident[:])

        def tr_k2(b, h):
            words = k2w[b][:].rearrange("p r l -> p (r l)").bitcast(F32)
            pair_transposes(("k2", b, h), words, (512 * h, 512 * h + 256))

        def ev_k2(b, h, eng):
            if h == 0:
                kg[b] = wide.tile([P, 4, P, 4], BF16, name="kg", align_bytes=64)
            dst = kg[b][:].rearrange("p r m e -> p (r m e)").bitcast(F32).rearrange("p (r m u) -> p r m u", r=4, u=2)
            evict_words(eng, dst[:, 2 * h : 2 * h + 2], psum["k2", b, h][:].rearrange("p a u r -> p a r u"))

        def q_k2(b):
            kcodes[b] = wide.tile([P, NB], U32, name="kcodes", align_bytes=64)
            kscales[b] = wide.tile([P, NB], U8, name="kscales", align_bytes=64)
            nc.vector.quantize_mx(out=kcodes[b][:].bitcast(FP8X4), scales=kscales[b][:], in_=kg[b][:].rearrange("p r m e -> p (r m e)"))

        def tr_d(g, h):
            pair_transposes(("d", g, h), dsb[g][:].bitcast(F32), (512 * h, 512 * h + 256))

        def ev_d(g, h, eng):
            if h == 0:
                dg[g] = keep.tile([P, 4, P, 4], BF16, name="dg%d" % g, align_bytes=64)
            dst = dg[g][:].rearrange("p r m e -> p (r m e)").bitcast(F32).rearrange("p (r m u) -> p r m u", r=4, u=2)
            evict_words(eng, dst[:, 2 * h : 2 * h + 2], psum["d", g, h][:].rearrange("p a u r -> p a r u"))

        def q_d(g):
            dcodes[g] = keep.tile([P, 512], U32, name="dcodes%d" % g, align_bytes=64)
            dscales[g] = keep.tile([P, 512], U8, name="dscales%d" % g, align_bytes=64)
            nc.vector.quantize_mx(out=dcodes[g][:].bitcast(FP8X4), scales=dscales[g][:], in_=dg[g][:].rearrange("p r m e -> p (r m e)"))

        def tr_k1(i):
            pair_transposes(("k1", i), k1sb[i][:].bitcast(F32), (0, 256))

        def ev_k1(i, eng):
            k1g[i] = keep.tile([P, 2, P, 4], BF16, name="k1g%d" % i, align_bytes=64)
            dst = k1g[i][:].rearrange("p g m e -> p (g m e)").bitcast(F32).rearrange("p (g m u) -> p g m u", g=2, u=2)
            evict_words(eng, dst, psum["k1", i][:].rearrange("p g u r -> p g r u"))

        def q_k1(i):
            k1codes[i] = keep.tile([P, 256], U32, name="k1codes%d" % i, align_bytes=64)
            k1scales[i] = keep.tile([P, 256], U8, name="k1scales%d" % i, align_bytes=64)
            nc.vector.quantize_mx(out=k1codes[i][:].bitcast(FP8X4), scales=k1scales[i][:], in_=k1g[i][:].rearrange("p g m e -> p (g m e)"))

        def mm1(b, g, t):
            ps = ps_g.tile([P, NB], F32, name="g_ps")
            psum["g", b, g, t] = ps
            cols = slice(t * P, (t + 1) * P)
            nc.tensor.matmul_mx(
                out=ps[:],
                lhsT=dcodes[g][:, cols].bitcast(FP8X4),
                lhsT_scale=dscales[g][:, cols],
                rhs=kcodes[b][:].bitcast(FP8X4),
                rhs_scale=kscales[b][:],
                start=True,
                stop=True,
            )

        def ev_g(b, g, t, eng):
            if t == 0:
                hp[b, g] = hpool.tile([P, 4, NB], BF16, name="hp", align_bytes=64)
            dst = hp[b, g][:, t, :]
            src = psum["g", b, g, t][:]
            col = polf[:, 4 * g + t : 4 * g + t + 1]
            if eng == "S":
                nc.scalar.activation(out=dst, in_=src, func=COPY, scale=col)
            else:
                nc.vector.tensor_scalar(out=dst, in0=src, scalar1=col, scalar2=None, op0=MULT)

        def inter(b, g, half, eng):
            if half == 0:
                hi[b, g] = hpool.tile([P, NB, 4], BF16, name="hi", align_bytes=64)
            cols = slice(half * 256, half * 256 + 256)
            dst = hi[b, g][:, cols, :].rearrange("p (c i) t -> p c t i", i=4)
            src = hp[b, g][:, :, cols].rearrange("p t (c i) -> p c t i", i=4)
            evict_words(eng, dst, src)

        def q_h(b, g):
            hcodes[b, g] = hcpool.tile([P, NB], U32, name="hcodes", align_bytes=64)
            hscales[b, g] = hcpool.tile([P, NB], U8, name="hscales", align_bytes=64)
            nc.vector.quantize_mx(
                out=hcodes[b, g][:].bitcast(FP8X4), scales=hscales[b, g][:], in_=hi[b, g][:].rearrange("p n t -> p (n t)")
            )

        def mm2(b, i):
            ps = ps_s.tile([P, NB], F32, name="s_ps")
            psum["s", b, i] = ps
            for g in range(GROUPS):
                cols = slice(g * P, (g + 1) * P)
                nc.tensor.matmul_mx(
                    out=ps[:],
                    lhsT=k1codes[i][:, cols].bitcast(FP8X4),
                    lhsT_scale=k1scales[i][:, cols],
                    rhs=hcodes[b, g][:].bitcast(FP8X4),
                    rhs_scale=hscales[b, g][:],
                    start=(g == 0),
                    stop=(g == GROUPS - 1),
                )

        def sub(b, i):
            res[b, i] = opool.tile([P, NB], F32, name="res")
            nc.vector.tensor_tensor(out=res[b, i][:], in0=psum["s", b, i][:], in1=dat[b, i // 4][:, i % 4, :], op=SUB)

        def mul_store(b, i, eng):
            if eng == "V":
                nc.vector.tensor_tensor(out=res[b, i][:], in0=res[b, i][:], in1=wt_bc[:, b * NB : (b + 1) * NB], op=MULT)
            else:
                for h in (0, 1):
                    c = slice(h * 256, h * 256 + 256)
                    nc.gpsimd.tensor_tensor(out=res[b, i][:, c], in0=res[b, i][:, c], in1=wt_bc[:, b * NB + h * 256 : b * NB + h * 256 + 256], op=MULT)
            nc.sync.dma_start(out=out[i * P : (i + 1) * P, b * NB : (b + 1) * NB], in_=res[b, i][:])

        def k2_prep(b, engs):
            tr_k2(b, 0)
            ev_k2(b, 0, engs[0])
            tr_k2(b, 1)
            ev_k2(b, 1, engs[1])
            q_k2(b)

        scale_bcast()
        nc.scalar.activation(out=polf[:], in_=polb[:], func=COPY)
        for r in range(4):
            widen(0, r)
        tr_k2(0, 0)
        ev_k2(0, 0, "S")
        tr_d(0, 0)
        ev_d(0, 0, "S")
        tr_k2(0, 1)
        ev_k2(0, 1, "S")
        tr_d(0, 1)
        ev_d(0, 1, "S")
        q_k2(0)
        q_d(0)
        tr_d(1, 0)
        ev_d(1, 0, "S")
        tr_d(1, 1)
        ev_d(1, 1, "S")
        q_d(1)

        def h_chain(b, g, evs, ints):
            for t in range(4):
                mm1(b, g, t)
                ev_g(b, g, t, evs[t])
            inter(b, g, 0, ints[0])
            inter(b, g, 1, ints[1])
            q_h(b, g)

        h_chain(0, 0, "SVSV", "VV")
        h_chain(0, 1, "SVSV", "VS")
        for i in range(2):
            tr_k1(i)
            ev_k1(i, "S")
            q_k1(i)
        for r in range(4):
            widen(1, r)
        k2_prep(1, "SS")
        INT = {(b, g): "SS" if g == 0 else "SV" for b in range(1, BLOCKS) for g in range(GROUPS)}
        for b in range(BLOCKS):
            nxt = b + 1 if b + 1 < BLOCKS else None
            nn = b + 2 if b + 2 < BLOCKS else None
            for i in range(ITILES):
                mm2(b, i)
                sub(b, i)
                if b == 0 and i + 2 < ITILES:
                    tr_k1(i + 2)
                    ev_k1(i + 2, "S")
                    q_k1(i + 2)
                if nxt is not None and i in (0, 2):
                    h_chain(nxt, i // 2, "SSSS", INT[nxt, i // 2])
                if nn is not None and i < 4:
                    widen(nn, i)
                if nn is not None and i == 5:
                    k2_prep(nn, "SS")
                mul_store(b, i, "V" if i % 3 == 2 or (b == 3 and i > 5) else "G")
